import numpy as np
import ml_dtypes


def mxq(x, axis, fmt="e4m3"):
    dtype, down = {"e4m3": (ml_dtypes.float8_e4m3fn, 7), "e5m2": (ml_dtypes.float8_e5m2, 14)}[fmt]
    v = np.moveaxis(np.asarray(x, np.float32).astype(ml_dtypes.bfloat16).astype(np.float64), axis, -1)
    blocks = v.reshape(v.shape[:-1] + (-1, 32))
    amax = np.abs(blocks).max(-1, keepdims=True)
    byte = np.maximum(np.where(amax > 0, np.frexp(amax)[1] - 1 + 127, 0) - down, 1)
    scale = np.exp2(byte - 127.0)
    codes = (blocks / scale).astype(np.float32).astype(dtype).astype(np.float64)
    return np.moveaxis((codes * scale).reshape(v.shape), -1, axis)


WIDE = False


def mx_kscale(k):
    if not WIDE:
        return np.ones(k)
    levels = np.array([10, -10, 5, -5, 0])
    if k % 512:
        return np.exp2(np.random.permutation(np.resize(levels, k // 32))).repeat(32)
    a = np.empty((k // 512, 16))
    for p in range(k // 512):
        a[p, :8] = np.random.permutation(np.resize(levels, 8))
        for g in range(8):
            far = levels[np.abs(levels - a[p, g]) >= 10]
            a[p, g + 8] = far[np.random.randint(len(far))]
    return np.exp2(a.ravel()).repeat(32)


def f64(x):
    return np.asarray(x).astype(np.float64)


def striped8(idx):
    return np.asarray(idx).reshape(8, -1, 16).transpose(0, 2, 1).reshape(128, -1).astype(np.uint16)


def unstriped8(offs):
    return offs.reshape(8, 16, -1).transpose(0, 2, 1).reshape(8, -1).astype(np.int64)


def pick8(x, idx, run):
    r = np.arange(len(x))
    return x[r[:, None], idx[r % (8 * run) // run]]


E2M1 = np.array([0.0, 0.5, 1.0, 1.5, 2.0, 3.0, 4.0, 6.0, -0.0, -0.5, -1.0, -1.5, -2.0, -3.0, -4.0, -6.0])


def pack_weight(w, fmt):
    k, n = w.shape
    w = f64(np.asarray(w, np.float32).astype(ml_dtypes.bfloat16)).reshape(k // 32, 32, n)
    amax = np.abs(w).max(1)
    if fmt == "e4m3":
        byte = np.frexp(amax)[1] - 1 + 127 - 7
    else:
        mant, ex = np.frexp(amax / 6.0)
        byte = np.where(mant > 0.5, ex, ex - 1) + 127
    byte = np.clip(np.where(amax > 0, byte, 1), 1, 254)
    scaled = (w * np.exp2(127.0 - byte)[:, None, :]).reshape(k, n).astype(np.float32)
    by_word = np.ascontiguousarray(scaled.reshape(k // 512, 128, 4, n).transpose(0, 1, 3, 2))
    if fmt == "e4m3":
        words = by_word.astype(ml_dtypes.float8_e4m3fn).view(np.uint8)
    else:
        c = by_word.astype(ml_dtypes.float4_e2m1fn).view(np.uint8) & 0xF
        words = (c[..., 0::2] | (c[..., 1::2] << 4)).reshape(k // 512, 128, 2 * n)
    return np.ascontiguousarray(words), np.ascontiguousarray(byte.astype(np.uint8).reshape(k // 512, 16, n))


def unpack_weight(words, scales, fmt):
    g, _, n = scales.shape
    words = np.ascontiguousarray(words).reshape(g, 128, n, -1)
    if fmt == "e4m3":
        vals = words.view(ml_dtypes.float8_e4m3fn).astype(np.float64)
    else:
        nib = np.empty((g, 128, n, 4), np.uint8)
        nib[..., 0::2] = words & 0xF
        nib[..., 1::2] = words >> 4
        vals = E2M1[nib]
    vals = vals * np.repeat(np.exp2(scales.astype(np.float64) - 127.0), 8, axis=1)[..., None]
    return vals.transpose(0, 1, 3, 2).reshape(g * 512, n)


D, E, T, Q, I = 512, 512, 1024, 128, 512


def setup_inputs():
    n = np.random.standard_normal
    idx = np.stack([np.random.permutation(T)[:I] for _ in range(8)])
    idx2 = np.stack([np.random.permutation(T)[:I] for _ in range(8)])
    fd = mx_kscale(D)
    fe = mx_kscale(E)
    keysp = pack_weight(n((D, T)) / fd[:, None], "e4m3")
    return {
        "query": (n((D, Q)) * 0.6 / np.sqrt(D) * fd[:, None]).astype(np.float32),
        "keys_words": keysp[0],
        "keys_scales": keysp[1],
        "gout": (n((E, Q)) * 1 / np.sqrt(E) * fe[:, None]).astype(np.float32),
        "vals": (n((E, T)) / fe[:, None]).astype(np.float32),
        "share": (np.random.uniform(0.4, 0.9, (Q, 1))).astype(np.float32),
        "fac": (np.random.uniform(0.5, 2.0, (1, T))).astype(np.float32),
        "old": (0.5 * n((Q, T))).astype(np.float32),
        "offs": striped8(idx),
        "offs2": striped8(idx2),
    }


def reference(query, keys_words, keys_scales, gout, vals, share, fac, old, offs, offs2):
    idx = unstriped8(offs)
    idx2 = unstriped8(offs2)
    keysu = unpack_weight(keys_words, keys_scales, "e4m3")
    queryq = mxq(f64(query), 0, "e4m3")
    a = queryq.T @ keysu
    dl = (pick8(a, idx2, 16) - pick8(a, idx, 16)) * f64(share)
    df0 = np.zeros((Q, T))
    df0[np.arange(Q)[:, None], idx[np.arange(Q) % 128 // 16]] = dl
    s = a + df0
    p = np.exp(s - np.max(s, axis=1, keepdims=True))
    z = np.sum(p, axis=1, keepdims=True)
    goutq = mxq(f64(gout), 0, "e4m3")
    valsq = mxq(f64(vals), 0, "e4m3")
    c0 = goutq.T @ valsq
    dz = np.sum(c0 * p * f64(fac) / np.square(z) * (-1.0), axis=1, keepdims=True)
    dp = c0 / z * f64(fac) + dz
    ds = dp * p
    ddl = pick8(ds, idx, 16)
    e1 = ddl * f64(share)
    s1 = np.zeros((Q, T))
    s1[np.arange(Q)[:, None], idx2[np.arange(Q) % 128 // 16]] = e1
    e2 = ddl * f64(share) * (-1.0)
    s2 = np.zeros((Q, T))
    s2[np.arange(Q)[:, None], idx[np.arange(Q) % 128 // 16]] = e2
    da = ds + s1 + s2
    y = da * 1024.0 + f64(old)
    return y

@@ -1,0 +1,284 @@
+from contextlib import ExitStack
+
+import concourse.mybir as mybir
+from concourse.masks import make_identity
+
+F32 = mybir.dt.float32
+BF16 = mybir.dt.bfloat16
+U32 = mybir.dt.uint32
+I32 = mybir.dt.int32
+U16 = mybir.dt.uint16
+U8 = mybir.dt.uint8
+FP8X4 = mybir.dt.float8_e4m3fn_x4
+ALU = mybir.AluOpType
+ACT = mybir.ActivationFunctionType
+
+P = 128
+PACK = 4
+T = 1024
+SLOTS = 512
+HALF = 512
+HALVES = T // HALF
+BLOCKS = HALF // P
+CHUNK = 256
+GRAD_SCALE = 1024.0
+FLOPS = 2 * 2 * 512 * 128 * 1024
+
+
+def interleaved(dst, src):
+    return (
+        dst.rearrange("p (c i t) -> p c t i", i=4, t=PACK),
+        src.rearrange("p t (c i) -> p c t i", i=4),
+    )
+
+
+def tile_attend_bborrowed_heads_kernel(
+    tc, query, keys_words, keys_scales, gout, vals, share, fac, old, offs, offs2, out
+):
+    nc = tc.nc
+    with ExitStack() as ctx:
+        sb = ctx.enter_context(tc.tile_pool(name="sb", bufs=1))
+        ps = ctx.enter_context(tc.psum_pool(name="ps", bufs=1))
+
+        def half(h):
+            return slice(h * HALF, (h + 1) * HALF)
+
+        def block(b):
+            return slice(b * P, (b + 1) * P)
+
+        q_raw = sb.tile([P, PACK, P], F32)
+        nc.sync.dma_start(out=q_raw[:], in_=query.rearrange("(p t) q -> p t q", t=PACK))
+        k_scales = sb.tile([P, T], U8, align_bytes=64)
+        for quad in range(4):
+            nc.sync.dma_start(
+                out=k_scales[32 * quad : 32 * quad + 4, :].bitcast(I32),
+                in_=keys_scales[0, 4 * quad : 4 * quad + 4, :].bitcast(I32),
+            )
+        k_hbm = keys_words[0].rearrange("p n t -> p (n t)")
+        k_words = []
+        for h in range(HALVES):
+            words = sb.tile([P, HALF], U32, align_bytes=64, name=f"k_words{h}")
+            nc.sync.dma_start(
+                out=words[:].bitcast(I32),
+                in_=k_hbm[:, h * HALF * PACK : (h + 1) * HALF * PACK].bitcast(I32),
+            )
+            k_words.append(words)
+        idx = sb.tile([P, SLOTS // 16], U16)
+        nc.sync.dma_start(idx[:], offs)
+        g_raw = sb.tile([P, PACK, P], F32)
+        nc.sync.dma_start(out=g_raw[:], in_=gout.rearrange("(p t) q -> p t q", t=PACK))
+        idx2 = sb.tile([P, SLOTS // 16], U16)
+        nc.sync.dma_start(idx2[:], offs2)
+        share_col = sb.tile([P, 1], F32)
+        nc.sync.dma_start(out=share_col[:], in_=share)
+        v_hbm = vals.rearrange("(p t) n -> p t n", t=PACK)
+        v_raw = []
+        for c in range(T // CHUNK):
+            raw = sb.tile([P, PACK, CHUNK], F32, name=f"v_raw{c}")
+            nc.sync.dma_start(out=raw[:], in_=v_hbm[:, :, c * CHUNK : (c + 1) * CHUNK])
+            v_raw.append(raw)
+        fac_rows = sb.tile([P, P], F32)
+        nc.gpsimd.memset(fac_rows[:], 0.0)
+        nc.sync.dma_start(
+            out=fac_rows[0 : T // P, :], in_=fac.rearrange("o (b n) -> (o b) n", n=P)
+        )
+        old_sb = sb.tile([P, T], F32)
+        nc.sync.dma_start(out=old_sb[:], in_=old)
+
+        ident = sb.tile([P, P], F32)
+        make_identity(nc, ident[:])
+
+        df0 = sb.tile([P, T], F32)
+        s1 = sb.tile([P, T], F32)
+        s2 = sb.tile([P, T], F32)
+        nc.vector.memset(df0[:], 0.0)
+        nc.vector.memset(s1[:], 0.0)
+        nc.vector.memset(s2[:], 0.0)
+
+        warm = sb.tile([P, 1], F32)
+        nc.scalar.activation(warm[:], df0[:, 0:1], ACT.Exp)
+
+        q_bf = sb.tile([P, P * PACK], BF16, align_bytes=64)
+        nc.vector.tensor_copy(*interleaved(q_bf[:], q_raw[:]))
+        q_codes = sb.tile([P, P], U32, align_bytes=64)
+        q_scales = sb.tile([P, P], U8, align_bytes=64)
+        nc.vector.quantize_mx(out=q_codes[:].bitcast(FP8X4), scales=q_scales[:], in_=q_bf[:])
+        a = sb.tile([P, T], F32)
+        pieces = (
+            (0, HALF, "rows0", nc.scalar.copy),
+            (HALF, CHUNK, "rows1", nc.vector.tensor_copy),
+            (HALF + CHUNK, CHUNK, "cf1", nc.scalar.copy),
+        )
+        for first, width, tag, copy in pieces:
+            bank = ps.tile([P, width], F32, tag=tag, name=f"a_bank{first}")
+            inside = first % HALF
+            nc.tensor.matmul_mx(
+                out=bank[:],
+                lhsT=q_codes[:].bitcast(FP8X4),
+                lhsT_scale=q_scales[:],
+                rhs=k_words[first // HALF][:, inside : inside + width].bitcast(FP8X4),
+                rhs_scale=k_scales[:, first : first + width],
+                start=True,
+                stop=True,
+            )
+            copy(a[:, first : first + width], bank[:])
+
+        g_bf = sb.tile([P, P * PACK], BF16, align_bytes=64)
+        nc.vector.tensor_copy(*interleaved(g_bf[:], g_raw[:]))
+        g_codes = sb.tile([P, P], U32, align_bytes=64)
+        g_scales = sb.tile([P, P], U8, align_bytes=64)
+        nc.vector.quantize_mx(out=g_codes[:].bitcast(FP8X4), scales=g_scales[:], in_=g_bf[:])
+
+        share_wide = sb.tile([P, SLOTS], F32)
+        nc.scalar.activation(share_wide[:], share_col[:].to_broadcast([P, SLOTS]), ACT.Copy)
+        neg_share_wide = sb.tile([P, SLOTS], F32)
+        nc.scalar.activation(
+            neg_share_wide[:], share_col[:].to_broadcast([P, SLOTS]), ACT.Copy, scale=-1.0
+        )
+        fac_bank = ps.tile([P, P], F32, tag="rows0")
+        nc.tensor.transpose(fac_bank[:], fac_rows[:], ident[:])
+        fac_cols = sb.tile([P, T // P], F32)
+        nc.scalar.copy(fac_cols[:], fac_bank[:, 0 : T // P])
+
+        v_bf = []
+        for h in range(HALVES):
+            bf = sb.tile([P, HALF * PACK], BF16, align_bytes=64, tag=f"v_bf{h}", name=f"v_bf{h}")
+            for c in range(HALF // CHUNK):
+                cols = slice(c * CHUNK * PACK, (c + 1) * CHUNK * PACK)
+                nc.scalar.copy(*interleaved(bf[:, cols], v_raw[h * (HALF // CHUNK) + c][:]))
+            v_bf.append(bf)
+
+        a_own = sb.tile([P, SLOTS], F32)
+        nc.vector.tensor_copy(a_own[:], a[:].indirect(idx[:]))
+
+        def move_scores(part, tag):
+            slots = slice(part * SLOTS // 2, (part + 1) * SLOTS // 2)
+            cols = slice(part * SLOTS // 32, (part + 1) * SLOTS // 32)
+            diff = sb.tile([P, SLOTS // 2], F32, align_bytes=64, tag=tag, name=f"diff{part}")
+            nc.vector.tensor_tensor(
+                diff[:], a[:].indirect(idx2[:, cols]), a_own[:, slots], ALU.subtract
+            )
+            nc.vector.tensor_tensor(
+                df0[:].indirect(idx[:, cols]), diff[:], share_wide[:, slots], ALU.mult
+            )
+
+        move_scores(0, "diff0")
+        cf = []
+        for h in range(HALVES):
+            v_codes = sb.tile([P, HALF], U32, align_bytes=64, name=f"v_codes{h}")
+            v_scales = sb.tile([P, HALF], U8, align_bytes=64, name=f"v_scales{h}")
+            nc.vector.quantize_mx(
+                out=v_codes[:].bitcast(FP8X4), scales=v_scales[:], in_=v_bf[h][:]
+            )
+            if h == 0:
+                move_scores(1, "v_bf0")
+            turned = ps.tile([P, HALF], F32, tag=f"turned{h}", name=f"c0t_bank{h}")
+            for b in range(BLOCKS):
+                nc.tensor.matmul_mx(
+                    out=turned[:, block(b)],
+                    lhsT=v_codes[:, block(b)].bitcast(FP8X4),
+                    lhsT_scale=v_scales[:, block(b)],
+                    rhs=g_codes[:].bitcast(FP8X4),
+                    rhs_scale=g_scales[:],
+                    start=True,
+                    stop=True,
+                )
+            cft = sb.tile([P, HALF], F32, name=f"cft{h}")
+            for b in range(BLOCKS):
+                col = h * BLOCKS + b
+                nc.scalar.activation(
+                    cft[:, block(b)], turned[:, block(b)], ACT.Copy,
+                    scale=fac_cols[:, col : col + 1],
+                )
+            cf_bank = ps.tile([P, HALF], F32, tag=f"cf{h}", name=f"cf_bank{h}")
+            for b in range(BLOCKS):
+                nc.tensor.transpose(cf_bank[:, block(b)], cft[:, block(b)], ident[:])
+            cf.append(cf_bank)
+
+        s = sb.tile([P, T], F32, align_bytes=64, tag="v_bf1")
+        neg_s = sb.tile([P, T], F32)
+        p = sb.tile([P, T], F32, tag="p")
+        cfp = sb.tile([P, T], F32)
+        neg_m = [sb.tile([P, 1], F32, name=f"neg_m{h}") for h in range(HALVES)]
+        z_part = [sb.tile([P, 1], F32, name=f"z_part{h}") for h in range(HALVES)]
+        w_part = [sb.tile([P, 1], F32, name=f"w_part{h}") for h in range(HALVES)]
+        for h in range(HALVES):
+            nc.vector.tensor_tensor(s[:, half(h)], a[:, half(h)], df0[:, half(h)], ALU.add)
+            nc.vector.tensor_scalar(
+                neg_s[:, half(h)], s[:, half(h)], -1.0, neg_m[0][:] if h else None,
+                ALU.mult, ALU.min, accum_out=neg_m[h][:],
+            )
+            nc.scalar.activation(
+                p[:, half(h)], neg_s[:, half(h)], ACT.Exp, bias=neg_m[h][:], scale=-1.0,
+                accum_out=z_part[h][:],
+            )
+        fix = sb.tile([P, 1], F32)
+        nc.scalar.activation(fix[:], neg_m[0][:], ACT.Exp, bias=neg_m[1][:], scale=-1.0)
+
+        nc.vector.scalar_tensor_tensor(
+            cfp[:, half(0)], cf[0][:], -1.0, p[:, half(0)], ALU.mult, ALU.mult,
+            accum_out=w_part[0][:],
+        )
+        z = sb.tile([P, 1], F32)
+        nc.vector.tensor_scalar(z[:], z_part[0][:], fix[:], z_part[1][:], ALU.mult, ALU.add)
+        rz = sb.tile([P, 1], F32)
+        nc.vector.reciprocal(rz[:], z[:])
+        nc.vector.scalar_tensor_tensor(
+            cfp[:, half(1)], cf[1][:], -1.0, p[:, half(1)], ALU.mult, ALU.mult,
+            accum_out=w_part[1][:],
+        )
+        rz_fix = sb.tile([P, 1], F32)
+        nc.scalar.activation(rz_fix[:], fix[:], ACT.Copy, scale=rz[:])
+        pn = sb.tile([P, T], F32)
+        nc.scalar.activation(pn[:, half(0)], p[:, half(0)], ACT.Copy, scale=rz_fix[:])
+        nc.scalar.activation(pn[:, half(1)], p[:, half(1)], ACT.Copy, scale=rz[:])
+        w0 = sb.tile([P, 1], F32)
+        nc.vector.tensor_scalar(w0[:], w_part[0][:], fix[:], rz[:], ALU.mult, ALU.mult)
+        shift = sb.tile([P, 1], F32)
+        nc.vector.tensor_scalar(shift[:], w_part[1][:], rz[:], w0[:], ALU.mult, ALU.add)
+        ds = sb.tile([P, T], F32)
+        for h in range(HALVES):
+            nc.vector.scalar_tensor_tensor(
+                ds[:, half(h)], cf[h][:], shift[:], pn[:, half(h)], ALU.add, ALU.mult
+            )
+
+        ddl = sb.tile([P, SLOTS], F32)
+        nc.vector.tensor_copy(ddl[:], ds[:].indirect(idx[:]))
+        nc.vector.tensor_tensor(s1[:].indirect(idx2[:]), ddl[:], share_wide[:], ALU.mult)
+        nc.vector.tensor_tensor(s2[:].indirect(idx[:]), ddl[:], neg_share_wide[:], ALU.mult)
+
+        old_small = sb.tile([P, T], F32, tag="p")
+        nc.scalar.activation(old_small[:], old_sb[:], ACT.Copy, scale=1.0 / GRAD_SCALE)
+        terms = (old_small, ds, s1)
+        sums = []
+        for h in range(HALVES):
+            sum_t = ps.tile([P, HALF], F32, tag=f"turned{h}", name=f"sum_bank{h}")
+            sums.append(sum_t)
+        for n, term in enumerate(terms):
+            for h in range(HALVES):
+                for b in range(BLOCKS):
+                    nc.tensor.matmul(
+                        sums[h][:, block(b)], term[:, block(h * BLOCKS + b)], ident[:],
+                        is_transpose=True,
+                        start=(n == 0 and b == 0),
+                        stop=(n == len(terms) - 1 and b == BLOCKS - 1),
+                    )
+        rests = []
+        for h in range(HALVES):
+            sum_sb = sb.tile([P, HALF], F32, name=f"sum_sb{h}")
+            nc.scalar.activation(sum_sb[:], sums[h][:], ACT.Copy, scale=GRAD_SCALE)
+            rest = ps.tile([P, HALF], F32, tag=f"rows{h}", name=f"rest_bank{h}")
+            for b in range(BLOCKS):
+                nc.tensor.transpose(rest[:, block(b)], sum_sb[:, block(b)], ident[:])
+            rests.append(rest)
+        for first, width, queue in (
+            (0, HALF, nc.sync), (HALF, CHUNK, nc.scalar), (HALF + CHUNK, CHUNK, nc.sync)
+        ):
+            cols = slice(first, first + width)
+            inside = first % HALF
+            res = sb.tile([P, width], F32, name=f"res{first}")
+            nc.vector.scalar_tensor_tensor(
+                res[:], s2[:, cols], GRAD_SCALE, rests[first // HALF][:, inside : inside + width],
+                ALU.mult, ALU.add,
+            )
+            queue.dma_start(out=out[:, cols], in_=res[:])

@@ -107,8 +107,9 @@ def tile_attend_bborrowed_heads_kernel(
         pieces = (
             (0, HALF, "rows0", nc.scalar.copy),
             (HALF, CHUNK, "rows1", nc.vector.tensor_copy),
-            (HALF + CHUNK, CHUNK, "cf1", nc.scalar.copy),
+            (HALF + CHUNK, CHUNK, "cf1", nc.vector.tensor_copy),
         )
+        a_banks = []
         for first, width, tag, copy in pieces:
             bank = ps.tile([P, width], F32, tag=tag, name=f"a_bank{first}")
             inside = first % HALF
@@ -122,20 +123,17 @@ def tile_attend_bborrowed_heads_kernel(
                 stop=True,
             )
             copy(a[:, first : first + width], bank[:])
+            a_banks.append(bank)
 
         g_bf = sb.tile([P, P * PACK], BF16, align_bytes=64)
-        nc.vector.tensor_copy(*interleaved(g_bf[:], g_raw[:]))
+        nc.scalar.copy(*interleaved(g_bf[:], g_raw[:]))
         g_codes = sb.tile([P, P], U32, align_bytes=64)
         g_scales = sb.tile([P, P], U8, align_bytes=64)
         nc.vector.quantize_mx(out=g_codes[:].bitcast(FP8X4), scales=g_scales[:], in_=g_bf[:])
 
         share_wide = sb.tile([P, SLOTS], F32)
         nc.scalar.activation(share_wide[:], share_col[:].to_broadcast([P, SLOTS]), ACT.Copy)
-        neg_share_wide = sb.tile([P, SLOTS], F32)
-        nc.scalar.activation(
-            neg_share_wide[:], share_col[:].to_broadcast([P, SLOTS]), ACT.Copy, scale=-1.0
-        )
-        fac_bank = ps.tile([P, P], F32, tag="rows0")
+        fac_bank = ps.tile([P, P], F32, tag="cf1")
         nc.tensor.transpose(fac_bank[:], fac_rows[:], ident[:])
         fac_cols = sb.tile([P, T // P], F32)
         nc.scalar.copy(fac_cols[:], fac_bank[:, 0 : T // P])
@@ -202,53 +200,60 @@ def tile_attend_bborrowed_heads_kernel(
         neg_m = [sb.tile([P, 1], F32, name=f"neg_m{h}") for h in range(HALVES)]
         z_part = [sb.tile([P, 1], F32, name=f"z_part{h}") for h in range(HALVES)]
         w_part = [sb.tile([P, 1], F32, name=f"w_part{h}") for h in range(HALVES)]
+        fix = sb.tile([P, 1], F32)
+        nc.vector.tensor_tensor(s[:, half(0)], a_banks[0][:], df0[:, half(0)], ALU.add)
+        nc.gpsimd.tensor_tensor(s[:, half(1)], a[:, half(1)], df0[:, half(1)], ALU.add)
         for h in range(HALVES):
-            nc.vector.tensor_tensor(s[:, half(h)], a[:, half(h)], df0[:, half(h)], ALU.add)
             nc.vector.tensor_scalar(
                 neg_s[:, half(h)], s[:, half(h)], -1.0, neg_m[0][:] if h else None,
                 ALU.mult, ALU.min, accum_out=neg_m[h][:],
             )
+            if h == 1:
+                nc.scalar.activation(fix[:], neg_m[0][:], ACT.Exp, bias=neg_m[1][:], scale=-1.0)
             nc.scalar.activation(
-                p[:, half(h)], neg_s[:, half(h)], ACT.Exp, bias=neg_m[h][:], scale=-1.0,
+                p[:, half(h)], s[:, half(h)], ACT.Exp, bias=neg_m[h][:],
                 accum_out=z_part[h][:],
             )
-        fix = sb.tile([P, 1], F32)
-        nc.scalar.activation(fix[:], neg_m[0][:], ACT.Exp, bias=neg_m[1][:], scale=-1.0)
 
         nc.vector.scalar_tensor_tensor(
             cfp[:, half(0)], cf[0][:], -1.0, p[:, half(0)], ALU.mult, ALU.mult,
             accum_out=w_part[0][:],
         )
+        w0 = sb.tile([P, 1], F32)
+        nc.scalar.activation(w0[:], w_part[0][:], ACT.Copy, scale=fix[:])
         z = sb.tile([P, 1], F32)
         nc.vector.tensor_scalar(z[:], z_part[0][:], fix[:], z_part[1][:], ALU.mult, ALU.add)
         rz = sb.tile([P, 1], F32)
         nc.vector.reciprocal(rz[:], z[:])
         nc.vector.scalar_tensor_tensor(
-            cfp[:, half(1)], cf[1][:], -1.0, p[:, half(1)], ALU.mult, ALU.mult,
+            cfp[:, half(1)], cf[1][:], rz[:], p[:, half(1)], ALU.mult, ALU.mult,
             accum_out=w_part[1][:],
         )
+        pn = sb.tile([P, T], F32)
+        nc.scalar.activation(pn[:, half(1)], p[:, half(1)], ACT.Copy, scale=rz[:])
         rz_fix = sb.tile([P, 1], F32)
         nc.scalar.activation(rz_fix[:], fix[:], ACT.Copy, scale=rz[:])
-        pn = sb.tile([P, T], F32)
         nc.scalar.activation(pn[:, half(0)], p[:, half(0)], ACT.Copy, scale=rz_fix[:])
-        nc.scalar.activation(pn[:, half(1)], p[:, half(1)], ACT.Copy, scale=rz[:])
-        w0 = sb.tile([P, 1], F32)
-        nc.vector.tensor_scalar(w0[:], w_part[0][:], fix[:], rz[:], ALU.mult, ALU.mult)
         shift = sb.tile([P, 1], F32)
-        nc.vector.tensor_scalar(shift[:], w_part[1][:], rz[:], w0[:], ALU.mult, ALU.add)
+        nc.vector.tensor_scalar(shift[:], w0[:], rz[:], w_part[1][:], ALU.mult, ALU.subtract)
         ds = sb.tile([P, T], F32)
-        for h in range(HALVES):
+        for h in (1, 0):
             nc.vector.scalar_tensor_tensor(
                 ds[:, half(h)], cf[h][:], shift[:], pn[:, half(h)], ALU.add, ALU.mult
             )
 
+        late = sb.tile([P, T + SLOTS], F32, tag="p")
+        old_small = late[:, 0:T]
+        neg_share_wide = late[:, T : T + SLOTS]
+        nc.scalar.activation(old_small, old_sb[:], ACT.Copy, scale=1.0 / GRAD_SCALE)
+        nc.scalar.activation(
+            neg_share_wide, share_col[:].to_broadcast([P, SLOTS]), ACT.Copy, scale=-1.0
+        )
         ddl = sb.tile([P, SLOTS], F32)
         nc.vector.tensor_copy(ddl[:], ds[:].indirect(idx[:]))
         nc.vector.tensor_tensor(s1[:].indirect(idx2[:]), ddl[:], share_wide[:], ALU.mult)
-        nc.vector.tensor_tensor(s2[:].indirect(idx[:]), ddl[:], neg_share_wide[:], ALU.mult)
+        nc.vector.tensor_tensor(s2[:].indirect(idx[:]), ddl[:], neg_share_wide, ALU.mult)
 
-        old_small = sb.tile([P, T], F32, tag="p")
-        nc.scalar.activation(old_small[:], old_sb[:], ACT.Copy, scale=1.0 / GRAD_SCALE)
         terms = (old_small, ds, s1)
         sums = []
         for h in range(HALVES):

@@ -15,21 +15,35 @@ ACT = mybir.ActivationFunctionType
 
 P = 128
 PACK = 4
+K = P * PACK
 T = 1024
 SLOTS = 512
+GROUP = 16
+LIST_COLS = SLOTS // GROUP
+QUADRANTS = 4
+SCALE_ROWS = 4
 HALF = 512
 HALVES = T // HALF
 BLOCKS = HALF // P
-CHUNK = 256
+QUARTER = HALF // 2
+LINE = 4
 GRAD_SCALE = 1024.0
-FLOPS = 2 * 2 * 512 * 128 * 1024
+FLOPS = 2 * 2 * K * P * T
 
 
 def interleaved(dst, src):
     return (
-        dst.rearrange("p (c i t) -> p c t i", i=4, t=PACK),
-        src.rearrange("p t (c i) -> p c t i", i=4),
+        dst.rearrange("p (c i r) -> p c r i", i=LINE, r=PACK),
+        src.rearrange("p r (c i) -> p c r i", i=LINE),
     )
+
+
+def half(h):
+    return slice(h * HALF, (h + 1) * HALF)
+
+
+def block(b):
+    return slice(b * P, (b + 1) * P)
 
 
 def tile_attend_bborrowed_heads_kernel(
@@ -40,21 +54,16 @@ def tile_attend_bborrowed_heads_kernel(
         sb = ctx.enter_context(tc.tile_pool(name="sb", bufs=1))
         ps = ctx.enter_context(tc.psum_pool(name="ps", bufs=1))
 
-        def half(h):
-            return slice(h * HALF, (h + 1) * HALF)
-
-        def block(b):
-            return slice(b * P, (b + 1) * P)
-
         q_raw = sb.tile([P, PACK, P], F32)
-        nc.sync.dma_start(out=q_raw[:], in_=query.rearrange("(p t) q -> p t q", t=PACK))
+        nc.sync.dma_start(out=q_raw[:], in_=query.rearrange("(p r) q -> p r q", r=PACK))
         k_scales = sb.tile([P, T], U8, align_bytes=64)
-        for quad in range(4):
+        for quad in range(QUADRANTS):
+            first_row = quad * (P // QUADRANTS)
             nc.sync.dma_start(
-                out=k_scales[32 * quad : 32 * quad + 4, :].bitcast(I32),
-                in_=keys_scales[0, 4 * quad : 4 * quad + 4, :].bitcast(I32),
+                out=k_scales[first_row : first_row + SCALE_ROWS, :].bitcast(I32),
+                in_=keys_scales[0, SCALE_ROWS * quad : SCALE_ROWS * (quad + 1), :].bitcast(I32),
             )
-        k_hbm = keys_words[0].rearrange("p n t -> p (n t)")
+        k_hbm = keys_words[0].rearrange("p t r -> p (t r)")
         k_words = []
         for h in range(HALVES):
             words = sb.tile([P, HALF], U32, align_bytes=64, name=f"k_words{h}")
@@ -63,19 +72,19 @@ def tile_attend_bborrowed_heads_kernel(
                 in_=k_hbm[:, h * HALF * PACK : (h + 1) * HALF * PACK].bitcast(I32),
             )
             k_words.append(words)
-        idx = sb.tile([P, SLOTS // 16], U16)
+        idx = sb.tile([P, LIST_COLS], U16)
         nc.sync.dma_start(idx[:], offs)
         g_raw = sb.tile([P, PACK, P], F32)
-        nc.sync.dma_start(out=g_raw[:], in_=gout.rearrange("(p t) q -> p t q", t=PACK))
-        idx2 = sb.tile([P, SLOTS // 16], U16)
+        nc.sync.dma_start(out=g_raw[:], in_=gout.rearrange("(p r) q -> p r q", r=PACK))
+        idx2 = sb.tile([P, LIST_COLS], U16)
         nc.sync.dma_start(idx2[:], offs2)
         share_col = sb.tile([P, 1], F32)
         nc.sync.dma_start(out=share_col[:], in_=share)
-        v_hbm = vals.rearrange("(p t) n -> p t n", t=PACK)
+        v_hbm = vals.rearrange("(p r) t -> p r t", r=PACK)
         v_raw = []
-        for c in range(T // CHUNK):
-            raw = sb.tile([P, PACK, CHUNK], F32, name=f"v_raw{c}")
-            nc.sync.dma_start(out=raw[:], in_=v_hbm[:, :, c * CHUNK : (c + 1) * CHUNK])
+        for c in range(T // QUARTER):
+            raw = sb.tile([P, PACK, QUARTER], F32, name=f"v_raw{c}")
+            nc.sync.dma_start(out=raw[:], in_=v_hbm[:, :, c * QUARTER : (c + 1) * QUARTER])
             v_raw.append(raw)
         fac_rows = sb.tile([P, P], F32)
         nc.gpsimd.memset(fac_rows[:], 0.0)
@@ -95,22 +104,14 @@ def tile_attend_bborrowed_heads_kernel(
         nc.vector.memset(s1[:], 0.0)
         nc.vector.memset(s2[:], 0.0)
 
-        warm = sb.tile([P, 1], F32)
-        nc.scalar.activation(warm[:], df0[:, 0:1], ACT.Exp)
-
-        q_bf = sb.tile([P, P * PACK], BF16, align_bytes=64)
+        q_bf = sb.tile([P, K], BF16, align_bytes=64)
         nc.vector.tensor_copy(*interleaved(q_bf[:], q_raw[:]))
         q_codes = sb.tile([P, P], U32, align_bytes=64)
         q_scales = sb.tile([P, P], U8, align_bytes=64)
         nc.vector.quantize_mx(out=q_codes[:].bitcast(FP8X4), scales=q_scales[:], in_=q_bf[:])
         a = sb.tile([P, T], F32)
-        pieces = (
-            (0, HALF, "rows0", nc.scalar.copy),
-            (HALF, CHUNK, "rows1", nc.vector.tensor_copy),
-            (HALF + CHUNK, CHUNK, "cf1", nc.vector.tensor_copy),
-        )
-        a_banks = []
-        for first, width, tag, copy in pieces:
+
+        def scores(first, width, tag, copy):
             bank = ps.tile([P, width], F32, tag=tag, name=f"a_bank{first}")
             inside = first % HALF
             nc.tensor.matmul_mx(
@@ -123,9 +124,13 @@ def tile_attend_bborrowed_heads_kernel(
                 stop=True,
             )
             copy(a[:, first : first + width], bank[:])
-            a_banks.append(bank)
+            return bank
 
-        g_bf = sb.tile([P, P * PACK], BF16, align_bytes=64)
+        a_bank0 = scores(0, HALF, "rows0", nc.scalar.copy)
+        scores(HALF, QUARTER, "rows1", nc.vector.tensor_copy)
+        scores(HALF + QUARTER, QUARTER, "cf1", nc.vector.tensor_copy)
+
+        g_bf = sb.tile([P, K], BF16, align_bytes=64)
         nc.scalar.copy(*interleaved(g_bf[:], g_raw[:]))
         g_codes = sb.tile([P, P], U32, align_bytes=64)
         g_scales = sb.tile([P, P], U8, align_bytes=64)
@@ -141,9 +146,9 @@ def tile_attend_bborrowed_heads_kernel(
         v_bf = []
         for h in range(HALVES):
             bf = sb.tile([P, HALF * PACK], BF16, align_bytes=64, tag=f"v_bf{h}", name=f"v_bf{h}")
-            for c in range(HALF // CHUNK):
-                cols = slice(c * CHUNK * PACK, (c + 1) * CHUNK * PACK)
-                nc.scalar.copy(*interleaved(bf[:, cols], v_raw[h * (HALF // CHUNK) + c][:]))
+            for c in range(HALF // QUARTER):
+                cols = slice(c * QUARTER * PACK, (c + 1) * QUARTER * PACK)
+                nc.scalar.copy(*interleaved(bf[:, cols], v_raw[h * (HALF // QUARTER) + c][:]))
             v_bf.append(bf)
 
         a_own = sb.tile([P, SLOTS], F32)
@@ -151,25 +156,24 @@ def tile_attend_bborrowed_heads_kernel(
 
         def move_scores(part, tag):
             slots = slice(part * SLOTS // 2, (part + 1) * SLOTS // 2)
-            cols = slice(part * SLOTS // 32, (part + 1) * SLOTS // 32)
+            entries = slice(part * LIST_COLS // 2, (part + 1) * LIST_COLS // 2)
             diff = sb.tile([P, SLOTS // 2], F32, align_bytes=64, tag=tag, name=f"diff{part}")
             nc.vector.tensor_tensor(
-                diff[:], a[:].indirect(idx2[:, cols]), a_own[:, slots], ALU.subtract
+                diff[:], a[:].indirect(idx2[:, entries]), a_own[:, slots], ALU.subtract
             )
             nc.vector.tensor_tensor(
-                df0[:].indirect(idx[:, cols]), diff[:], share_wide[:, slots], ALU.mult
+                df0[:].indirect(idx[:, entries]), diff[:], share_wide[:, slots], ALU.mult
             )
 
-        move_scores(0, "diff0")
-        cf = []
-        for h in range(HALVES):
+        def quantise_values(h):
             v_codes = sb.tile([P, HALF], U32, align_bytes=64, name=f"v_codes{h}")
             v_scales = sb.tile([P, HALF], U8, align_bytes=64, name=f"v_scales{h}")
             nc.vector.quantize_mx(
                 out=v_codes[:].bitcast(FP8X4), scales=v_scales[:], in_=v_bf[h][:]
             )
-            if h == 0:
-                move_scores(1, "v_bf0")
+            return v_codes, v_scales
+
+        def weighted_product(h, v_codes, v_scales):
             turned = ps.tile([P, HALF], F32, tag=f"turned{h}", name=f"c0t_bank{h}")
             for b in range(BLOCKS):
                 nc.tensor.matmul_mx(
@@ -191,7 +195,13 @@ def tile_attend_bborrowed_heads_kernel(
             cf_bank = ps.tile([P, HALF], F32, tag=f"cf{h}", name=f"cf_bank{h}")
             for b in range(BLOCKS):
                 nc.tensor.transpose(cf_bank[:, block(b)], cft[:, block(b)], ident[:])
-            cf.append(cf_bank)
+            return cf_bank
+
+        move_scores(0, "diff0")
+        values0 = quantise_values(0)
+        move_scores(1, "v_bf0")
+        cf = [weighted_product(0, *values0)]
+        cf.append(weighted_product(1, *quantise_values(1)))
 
         s = sb.tile([P, T], F32, align_bytes=64, tag="v_bf1")
         neg_s = sb.tile([P, T], F32)
@@ -201,19 +211,26 @@ def tile_attend_bborrowed_heads_kernel(
         z_part = [sb.tile([P, 1], F32, name=f"z_part{h}") for h in range(HALVES)]
         w_part = [sb.tile([P, 1], F32, name=f"w_part{h}") for h in range(HALVES)]
         fix = sb.tile([P, 1], F32)
-        nc.vector.tensor_tensor(s[:, half(0)], a_banks[0][:], df0[:, half(0)], ALU.add)
+        nc.vector.tensor_tensor(s[:, half(0)], a_bank0[:], df0[:, half(0)], ALU.add)
         nc.gpsimd.tensor_tensor(s[:, half(1)], a[:, half(1)], df0[:, half(1)], ALU.add)
-        for h in range(HALVES):
+
+        def negated_maximum(h, start):
             nc.vector.tensor_scalar(
-                neg_s[:, half(h)], s[:, half(h)], -1.0, neg_m[0][:] if h else None,
+                neg_s[:, half(h)], s[:, half(h)], -1.0, start,
                 ALU.mult, ALU.min, accum_out=neg_m[h][:],
             )
-            if h == 1:
-                nc.scalar.activation(fix[:], neg_m[0][:], ACT.Exp, bias=neg_m[1][:], scale=-1.0)
+
+        def exponentials(h):
             nc.scalar.activation(
                 p[:, half(h)], s[:, half(h)], ACT.Exp, bias=neg_m[h][:],
                 accum_out=z_part[h][:],
             )
+
+        negated_maximum(0, None)
+        exponentials(0)
+        negated_maximum(1, neg_m[0][:])
+        nc.scalar.activation(fix[:], neg_m[0][:], ACT.Exp, bias=neg_m[1][:], scale=-1.0)
+        exponentials(1)
 
         nc.vector.scalar_tensor_tensor(
             cfp[:, half(0)], cf[0][:], -1.0, p[:, half(0)], ALU.mult, ALU.mult,
@@ -237,7 +254,7 @@ def tile_attend_bborrowed_heads_kernel(
         shift = sb.tile([P, 1], F32)
         nc.vector.tensor_scalar(shift[:], w0[:], rz[:], w_part[1][:], ALU.mult, ALU.subtract)
         ds = sb.tile([P, T], F32)
-        for h in (1, 0):
+        for h in reversed(range(HALVES)):
             nc.vector.scalar_tensor_tensor(
                 ds[:, half(h)], cf[h][:], shift[:], pn[:, half(h)], ALU.add, ALU.mult
             )
@@ -255,10 +272,9 @@ def tile_attend_bborrowed_heads_kernel(
         nc.vector.tensor_tensor(s2[:].indirect(idx[:]), ddl[:], neg_share_wide, ALU.mult)
 
         terms = (old_small, ds, s1)
-        sums = []
-        for h in range(HALVES):
-            sum_t = ps.tile([P, HALF], F32, tag=f"turned{h}", name=f"sum_bank{h}")
-            sums.append(sum_t)
+        sums = [
+            ps.tile([P, HALF], F32, tag=f"turned{h}", name=f"sum_bank{h}") for h in range(HALVES)
+        ]
         for n, term in enumerate(terms):
             for h in range(HALVES):
                 for b in range(BLOCKS):
@@ -276,8 +292,11 @@ def tile_attend_bborrowed_heads_kernel(
             for b in range(BLOCKS):
                 nc.tensor.transpose(rest[:, block(b)], sum_sb[:, block(b)], ident[:])
             rests.append(rest)
+
         for first, width, queue in (
-            (0, HALF, nc.sync), (HALF, CHUNK, nc.scalar), (HALF + CHUNK, CHUNK, nc.sync)
+            (0, HALF, nc.sync),
+            (HALF, QUARTER, nc.scalar),
+            (HALF + QUARTER, QUARTER, nc.sync),
         ):
             cols = slice(first, first + width)
             inside = first % HALF

from contextlib import ExitStack

import concourse.mybir as mybir
from concourse.masks import make_identity

F32 = mybir.dt.float32
BF16 = mybir.dt.bfloat16
U32 = mybir.dt.uint32
I32 = mybir.dt.int32
U16 = mybir.dt.uint16
U8 = mybir.dt.uint8
FP8X4 = mybir.dt.float8_e4m3fn_x4
ALU = mybir.AluOpType
ACT = mybir.ActivationFunctionType

P = 128
PACK = 4
K = P * PACK
T = 1024
SLOTS = 512
GROUP = 16
LIST_COLS = SLOTS // GROUP
QUADRANTS = 4
SCALE_ROWS = 4
HALF = 512
HALVES = T // HALF
BLOCKS = HALF // P
QUARTER = HALF // 2
LINE = 4
GRAD_SCALE = 1024.0
FLOPS = 2 * 2 * K * P * T


def interleaved(dst, src):
    return (
        dst.rearrange("p (c i r) -> p c r i", i=LINE, r=PACK),
        src.rearrange("p r (c i) -> p c r i", i=LINE),
    )


def half(h):
    return slice(h * HALF, (h + 1) * HALF)


def block(b):
    return slice(b * P, (b + 1) * P)


def tile_attend_bborrowed_heads_kernel(
    tc, query, keys_words, keys_scales, gout, vals, share, fac, old, offs, offs2, out
):
    nc = tc.nc
    with ExitStack() as ctx:
        sb = ctx.enter_context(tc.tile_pool(name="sb", bufs=1))
        ps = ctx.enter_context(tc.psum_pool(name="ps", bufs=1))

        q_raw = sb.tile([P, PACK, P], F32)
        nc.sync.dma_start(out=q_raw[:], in_=query.rearrange("(p r) q -> p r q", r=PACK))
        k_scales = sb.tile([P, T], U8, align_bytes=64)
        for quad in range(QUADRANTS):
            first_row = quad * (P // QUADRANTS)
            nc.sync.dma_start(
                out=k_scales[first_row : first_row + SCALE_ROWS, :].bitcast(I32),
                in_=keys_scales[0, SCALE_ROWS * quad : SCALE_ROWS * (quad + 1), :].bitcast(I32),
            )
        k_hbm = keys_words[0].rearrange("p t r -> p (t r)")
        k_words = []
        for h in range(HALVES):
            words = sb.tile([P, HALF], U32, align_bytes=64, name=f"k_words{h}")
            nc.sync.dma_start(
                out=words[:].bitcast(I32),
                in_=k_hbm[:, h * HALF * PACK : (h + 1) * HALF * PACK].bitcast(I32),
            )
            k_words.append(words)
        idx = sb.tile([P, LIST_COLS], U16)
        nc.sync.dma_start(idx[:], offs)
        g_raw = sb.tile([P, PACK, P], F32)
        nc.sync.dma_start(out=g_raw[:], in_=gout.rearrange("(p r) q -> p r q", r=PACK))
        idx2 = sb.tile([P, LIST_COLS], U16)
        nc.sync.dma_start(idx2[:], offs2)
        share_col = sb.tile([P, 1], F32)
        nc.sync.dma_start(out=share_col[:], in_=share)
        v_hbm = vals.rearrange("(p r) t -> p r t", r=PACK)
        v_raw = []
        for c in range(T // QUARTER):
            raw = sb.tile([P, PACK, QUARTER], F32, name=f"v_raw{c}")
            nc.sync.dma_start(out=raw[:], in_=v_hbm[:, :, c * QUARTER : (c + 1) * QUARTER])
            v_raw.append(raw)
        fac_rows = sb.tile([P, P], F32)
        nc.gpsimd.memset(fac_rows[:], 0.0)
        nc.sync.dma_start(
            out=fac_rows[0 : T // P, :], in_=fac.rearrange("o (b n) -> (o b) n", n=P)
        )
        old_sb = sb.tile([P, T], F32)
        nc.sync.dma_start(out=old_sb[:], in_=old)

        ident = sb.tile([P, P], F32)
        make_identity(nc, ident[:])

        df0 = sb.tile([P, T], F32)
        s1 = sb.tile([P, T], F32)
        s2 = sb.tile([P, T], F32)
        nc.vector.memset(df0[:], 0.0)
        nc.vector.memset(s1[:], 0.0)
        nc.vector.memset(s2[:], 0.0)

        q_bf = sb.tile([P, K], BF16, align_bytes=64)
        nc.vector.tensor_copy(*interleaved(q_bf[:], q_raw[:]))
        q_codes = sb.tile([P, P], U32, align_bytes=64)
        q_scales = sb.tile([P, P], U8, align_bytes=64)
        nc.vector.quantize_mx(out=q_codes[:].bitcast(FP8X4), scales=q_scales[:], in_=q_bf[:])
        a = sb.tile([P, T], F32)

        def scores(first, width, tag, copy):
            bank = ps.tile([P, width], F32, tag=tag, name=f"a_bank{first}")
            inside = first % HALF
            nc.tensor.matmul_mx(
                out=bank[:],
                lhsT=q_codes[:].bitcast(FP8X4),
                lhsT_scale=q_scales[:],
                rhs=k_words[first // HALF][:, inside : inside + width].bitcast(FP8X4),
                rhs_scale=k_scales[:, first : first + width],
                start=True,
                stop=True,
            )
            copy(a[:, first : first + width], bank[:])
            return bank

        a_bank0 = scores(0, HALF, "rows0", nc.scalar.copy)
        scores(HALF, QUARTER, "rows1", nc.vector.tensor_copy)
        scores(HALF + QUARTER, QUARTER, "cf1", nc.vector.tensor_copy)

        g_bf = sb.tile([P, K], BF16, align_bytes=64)
        nc.scalar.copy(*interleaved(g_bf[:], g_raw[:]))
        g_codes = sb.tile([P, P], U32, align_bytes=64)
        g_scales = sb.tile([P, P], U8, align_bytes=64)
        nc.vector.quantize_mx(out=g_codes[:].bitcast(FP8X4), scales=g_scales[:], in_=g_bf[:])

        share_wide = sb.tile([P, SLOTS], F32)
        nc.scalar.activation(share_wide[:], share_col[:].to_broadcast([P, SLOTS]), ACT.Copy)
        fac_bank = ps.tile([P, P], F32, tag="cf1")
        nc.tensor.transpose(fac_bank[:], fac_rows[:], ident[:])
        fac_cols = sb.tile([P, T // P], F32)
        nc.scalar.copy(fac_cols[:], fac_bank[:, 0 : T // P])

        v_bf = []
        for h in range(HALVES):
            bf = sb.tile([P, HALF * PACK], BF16, align_bytes=64, tag=f"v_bf{h}", name=f"v_bf{h}")
            for c in range(HALF // QUARTER):
                cols = slice(c * QUARTER * PACK, (c + 1) * QUARTER * PACK)
                nc.scalar.copy(*interleaved(bf[:, cols], v_raw[h * (HALF // QUARTER) + c][:]))
            v_bf.append(bf)

        a_own = sb.tile([P, SLOTS], F32)
        nc.vector.tensor_copy(a_own[:], a[:].indirect(idx[:]))

        def move_scores(part, tag):
            slots = slice(part * SLOTS // 2, (part + 1) * SLOTS // 2)
            entries = slice(part * LIST_COLS // 2, (part + 1) * LIST_COLS // 2)
            diff = sb.tile([P, SLOTS // 2], F32, align_bytes=64, tag=tag, name=f"diff{part}")
            nc.vector.tensor_tensor(
                diff[:], a[:].indirect(idx2[:, entries]), a_own[:, slots], ALU.subtract
            )
            nc.vector.tensor_tensor(
                df0[:].indirect(idx[:, entries]), diff[:], share_wide[:, slots], ALU.mult
            )

        def quantise_values(h):
            v_codes = sb.tile([P, HALF], U32, align_bytes=64, name=f"v_codes{h}")
            v_scales = sb.tile([P, HALF], U8, align_bytes=64, name=f"v_scales{h}")
            nc.vector.quantize_mx(
                out=v_codes[:].bitcast(FP8X4), scales=v_scales[:], in_=v_bf[h][:]
            )
            return v_codes, v_scales

        def weighted_product(h, v_codes, v_scales):
            turned = ps.tile([P, HALF], F32, tag=f"turned{h}", name=f"c0t_bank{h}")
            for b in range(BLOCKS):
                nc.tensor.matmul_mx(
                    out=turned[:, block(b)],
                    lhsT=v_codes[:, block(b)].bitcast(FP8X4),
                    lhsT_scale=v_scales[:, block(b)],
                    rhs=g_codes[:].bitcast(FP8X4),
                    rhs_scale=g_scales[:],
                    start=True,
                    stop=True,
                )
            cft = sb.tile([P, HALF], F32, name=f"cft{h}")
            for b in range(BLOCKS):
                col = h * BLOCKS + b
                nc.scalar.activation(
                    cft[:, block(b)], turned[:, block(b)], ACT.Copy,
                    scale=fac_cols[:, col : col + 1],
                )
            cf_bank = ps.tile([P, HALF], F32, tag=f"cf{h}", name=f"cf_bank{h}")
            for b in range(BLOCKS):
                nc.tensor.transpose(cf_bank[:, block(b)], cft[:, block(b)], ident[:])
            return cf_bank

        move_scores(0, "diff0")
        values0 = quantise_values(0)
        move_scores(1, "v_bf0")
        cf = [weighted_product(0, *values0)]
        cf.append(weighted_product(1, *quantise_values(1)))

        s = sb.tile([P, T], F32, align_bytes=64, tag="v_bf1")
        neg_s = sb.tile([P, T], F32)
        p = sb.tile([P, T], F32, tag="p")
        cfp = sb.tile([P, T], F32)
        neg_m = [sb.tile([P, 1], F32, name=f"neg_m{h}") for h in range(HALVES)]
        z_part = [sb.tile([P, 1], F32, name=f"z_part{h}") for h in range(HALVES)]
        w_part = [sb.tile([P, 1], F32, name=f"w_part{h}") for h in range(HALVES)]
        fix = sb.tile([P, 1], F32)
        nc.vector.tensor_tensor(s[:, half(0)], a_bank0[:], df0[:, half(0)], ALU.add)
        nc.gpsimd.tensor_tensor(s[:, half(1)], a[:, half(1)], df0[:, half(1)], ALU.add)

        def negated_maximum(h, start):
            nc.vector.tensor_scalar(
                neg_s[:, half(h)], s[:, half(h)], -1.0, start,
                ALU.mult, ALU.min, accum_out=neg_m[h][:],
            )

        def exponentials(h):
            nc.scalar.activation(
                p[:, half(h)], s[:, half(h)], ACT.Exp, bias=neg_m[h][:],
                accum_out=z_part[h][:],
            )

        negated_maximum(0, None)
        exponentials(0)
        negated_maximum(1, neg_m[0][:])
        nc.scalar.activation(fix[:], neg_m[0][:], ACT.Exp, bias=neg_m[1][:], scale=-1.0)
        exponentials(1)

        nc.vector.scalar_tensor_tensor(
            cfp[:, half(0)], cf[0][:], -1.0, p[:, half(0)], ALU.mult, ALU.mult,
            accum_out=w_part[0][:],
        )
        w0 = sb.tile([P, 1], F32)
        nc.scalar.activation(w0[:], w_part[0][:], ACT.Copy, scale=fix[:])
        z = sb.tile([P, 1], F32)
        nc.vector.tensor_scalar(z[:], z_part[0][:], fix[:], z_part[1][:], ALU.mult, ALU.add)
        rz = sb.tile([P, 1], F32)
        nc.vector.reciprocal(rz[:], z[:])
        nc.vector.scalar_tensor_tensor(
            cfp[:, half(1)], cf[1][:], rz[:], p[:, half(1)], ALU.mult, ALU.mult,
            accum_out=w_part[1][:],
        )
        pn = sb.tile([P, T], F32)
        nc.scalar.activation(pn[:, half(1)], p[:, half(1)], ACT.Copy, scale=rz[:])
        rz_fix = sb.tile([P, 1], F32)
        nc.scalar.activation(rz_fix[:], fix[:], ACT.Copy, scale=rz[:])
        nc.scalar.activation(pn[:, half(0)], p[:, half(0)], ACT.Copy, scale=rz_fix[:])
        shift = sb.tile([P, 1], F32)
        nc.vector.tensor_scalar(shift[:], w0[:], rz[:], w_part[1][:], ALU.mult, ALU.subtract)
        ds = sb.tile([P, T], F32)
        for h in reversed(range(HALVES)):
            nc.vector.scalar_tensor_tensor(
                ds[:, half(h)], cf[h][:], shift[:], pn[:, half(h)], ALU.add, ALU.mult
            )

        late = sb.tile([P, T + SLOTS], F32, tag="p")
        old_small = late[:, 0:T]
        neg_share_wide = late[:, T : T + SLOTS]
        nc.scalar.activation(old_small, old_sb[:], ACT.Copy, scale=1.0 / GRAD_SCALE)
        nc.scalar.activation(
            neg_share_wide, share_col[:].to_broadcast([P, SLOTS]), ACT.Copy, scale=-1.0
        )
        ddl = sb.tile([P, SLOTS], F32)
        nc.vector.tensor_copy(ddl[:], ds[:].indirect(idx[:]))
        nc.vector.tensor_tensor(s1[:].indirect(idx2[:]), ddl[:], share_wide[:], ALU.mult)
        nc.vector.tensor_tensor(s2[:].indirect(idx[:]), ddl[:], neg_share_wide, ALU.mult)

        terms = (old_small, ds, s1)
        sums = [
            ps.tile([P, HALF], F32, tag=f"turned{h}", name=f"sum_bank{h}") for h in range(HALVES)
        ]
        for n, term in enumerate(terms):
            for h in range(HALVES):
                for b in range(BLOCKS):
                    nc.tensor.matmul(
                        sums[h][:, block(b)], term[:, block(h * BLOCKS + b)], ident[:],
                        is_transpose=True,
                        start=(n == 0 and b == 0),
                        stop=(n == len(terms) - 1 and b == BLOCKS - 1),
                    )
        rests = []
        for h in range(HALVES):
            sum_sb = sb.tile([P, HALF], F32, name=f"sum_sb{h}")
            nc.scalar.activation(sum_sb[:], sums[h][:], ACT.Copy, scale=GRAD_SCALE)
            rest = ps.tile([P, HALF], F32, tag=f"rows{h}", name=f"rest_bank{h}")
            for b in range(BLOCKS):
                nc.tensor.transpose(rest[:, block(b)], sum_sb[:, block(b)], ident[:])
            rests.append(rest)

        for first, width, queue in (
            (0, HALF, nc.sync),
            (HALF, QUARTER, nc.scalar),
            (HALF + QUARTER, QUARTER, nc.sync),
        ):
            cols = slice(first, first + width)
            inside = first % HALF
            res = sb.tile([P, width], F32, name=f"res{first}")
            nc.vector.scalar_tensor_tensor(
                res[:], s2[:, cols], GRAD_SCALE, rests[first // HALF][:, inside : inside + width],
                ALU.mult, ALU.add,
            )
            queue.dma_start(out=out[:, cols], in_=res[:])
